import numpy as np
import ml_dtypes


def mxq(x, axis, fmt="e4m3"):
    dtype, down = {"e4m3": (ml_dtypes.float8_e4m3fn, 7), "e5m2": (ml_dtypes.float8_e5m2, 14)}[fmt]
    v = np.moveaxis(np.asarray(x, np.float32).astype(ml_dtypes.bfloat16).astype(np.float64), axis, -1)
    blocks = v.reshape(v.shape[:-1] + (-1, 32))
    amax = np.abs(blocks).max(-1, keepdims=True)
    byte = np.maximum(np.where(amax > 0, np.frexp(amax)[1] - 1 + 127, 0) - down, 1)
    scale = np.exp2(byte - 127.0)
    codes = (blocks / scale).astype(np.float32).astype(dtype).astype(np.float64)
    return np.moveaxis((codes * scale).reshape(v.shape), -1, axis)


WIDE = False


def mx_kscale(k):
    if not WIDE:
        return np.ones(k)
    levels = np.array([30, -30])
    if k % 512:
        return np.exp2(np.random.permutation(np.resize(levels, k // 32))).repeat(32)
    a = np.empty((k // 512, 16))
    for p in range(k // 512):
        a[p, :8] = np.random.permutation(np.resize(levels, 8))
        for g in range(8):
            far = levels[np.abs(levels - a[p, g]) >= 10]
            a[p, g + 8] = far[np.random.randint(len(far))]
    return np.exp2(a.ravel()).repeat(32)


def f64(x):
    return np.asarray(x).astype(np.float64)


def planes(y):
    n, m = y.shape
    v = y.astype(np.float32).astype(ml_dtypes.bfloat16).astype(np.float64).reshape(n // 32, 32, m)
    top = np.abs(v).max(1)
    byte = np.clip(np.where(top > 0, np.frexp(top)[1] - 1 + 127 - 7, 1), 1, 254)
    codes = (v * np.exp2(127.0 - byte)[:, None, :]).reshape(n, m).astype(np.float32).astype(ml_dtypes.float8_e4m3fn).view(np.uint8)
    words = codes.reshape(n // 512, 128, 4, m).transpose(0, 1, 3, 2)
    return np.ascontiguousarray(words), np.ascontiguousarray(byte.astype(np.uint8).reshape(n // 512, 16, m))


K, M, T = 1024, 1024, 1024


def setup_inputs():
    n = np.random.standard_normal
    s1 = mx_kscale(K)[:, None]
    s2 = mx_kscale(K)[:, None]
    return {
        "w": (n((K, M)) / np.sqrt(K) * s1).astype(np.float32),
        "xd": (n((K, T)) / s1).astype(np.float32),
        "wd": (n((K, M)) / np.sqrt(K) * s2).astype(np.float32),
        "x": (n((K, T)) / s2).astype(np.float32),
        "r": (n((1024, 1024))).astype(np.float32),
    }


def reference(w, xd, wd, x, r):
    w_ = mxq(f64(w), 0, "e4m3")
    xd_ = mxq(f64(xd), 0, "e5m2")
    wd_ = mxq(f64(wd), 0, "e5m2")
    x_ = mxq(f64(x), 0, "e4m3")
    y = w_.T @ xd_ + wd_.T @ x_
    out_0 = f64(r) + y
    return (out_0,) + planes(out_0)

@@ -1,0 +1,174 @@
+from contextlib import ExitStack
+
+import concourse.mybir as mybir
+
+K, M, T = 1024, 1024, 1024
+FLOPS = 2 * 2 * K * M * T
+
+F32 = mybir.dt.float32
+BF16 = mybir.dt.bfloat16
+U32 = mybir.dt.uint32
+I32 = mybir.dt.int32
+U8 = mybir.dt.uint8
+E4M3 = mybir.dt.float8_e4m3fn_x4
+E5M2 = mybir.dt.float8_e5m2_x4
+
+P = 128
+PACK = 4
+SPAN = P * PACK
+N_TILE = 512
+K_PASSES = K // SPAN
+ROW_GROUPS = M // SPAN
+COL_HALVES = T // N_TILE
+SCALAR_COLUMNS = 48
+ROW_PAIR = 2
+
+
+def tile_mix_jvp_fm_pl_res_kernel(tc, w, xd, wd, x, r, out_0, out_1, out_2):
+    nc = tc.nc
+    products = [(w, E4M3, xd, E5M2), (wd, E5M2, x, E4M3)]
+    passes = [(q, g) for q in range(len(products)) for g in range(K_PASSES)]
+
+    with ExitStack() as ctx:
+        keep = ctx.enter_context(tc.tile_pool(name="keep", bufs=1))
+        stage = ctx.enter_context(tc.tile_pool(name="stage", bufs=4))
+        psum = ctx.enter_context(tc.psum_pool(name="psum", bufs=1))
+        ctx.enter_context(tc.manual_schedule())
+
+        def rows_on_partitions(dram, first_row):
+            return dram[first_row : first_row + SPAN, :].rearrange("(p j) c -> p j c", j=PACK)
+
+        weight_raw, moving_raw, result = {}, {}, {}
+
+        def load_weight(a, q, g):
+            raw = keep.tile([P, PACK, SPAN], F32, name="weight_raw_%d_%d_%d" % (a, q, g))
+            rows = rows_on_partitions(products[q][0], g * SPAN)
+            nc.sync.dma_start(out=raw[:], in_=rows[:, :, a * SPAN : (a + 1) * SPAN])
+            weight_raw[a, q, g] = raw
+
+        def load_moving(q, g):
+            raw = keep.tile([P, PACK, T], F32, name="moving_raw_%d_%d" % (q, g))
+            nc.sync.dma_start(out=raw[:], in_=rows_on_partitions(products[q][2], g * SPAN))
+            moving_raw[q, g] = raw
+
+        def load_residual(a):
+            res = keep.tile([P, PACK, T], F32, name="result_%d" % a)
+            rows = rows_on_partitions(r, a * SPAN)
+            for i0 in range(0, PACK, ROW_PAIR):
+                nc.sync.dma_start(out=res[:, i0 : i0 + ROW_PAIR, :], in_=rows[:, i0 : i0 + ROW_PAIR, :])
+            result[a] = res
+
+        for q, g in passes:
+            load_weight(0, q, g)
+            load_moving(q, g)
+        load_residual(0)
+        for q, g in passes:
+            load_weight(1, q, g)
+        load_residual(1)
+
+        def copy_on(engine, out, in_):
+            if engine == "vector":
+                nc.vector.tensor_copy(out=out, in_=in_)
+            else:
+                nc.scalar.copy(out=out, in_=in_)
+
+        def interleave(engine, rows):
+            grouped = stage.tile([P, N_TILE * PACK], BF16, name="grouped", align_bytes=64)
+            copy_on(
+                engine,
+                grouped[:].rearrange("p (c u j) -> p c j u", u=4, j=PACK),
+                rows.rearrange("p j (c u) -> p c j u", u=4),
+            )
+            return grouped
+
+        def quantise(grouped, codes, scales, fmt):
+            nc.vector.quantize_mx(out=codes.bitcast(fmt), scales=scales, in_=grouped[:])
+
+        weight_mx, moving_mx, banks = {}, {}, {}
+
+        def quantise_weight(a, q, g):
+            grouped = stage.tile([P, SPAN * PACK], BF16, name="grouped", align_bytes=64)
+            dst = grouped[:].rearrange("p (i m j) -> p m i j", i=PACK, j=PACK)
+            src = weight_raw[a, q, g][:].rearrange("p j (m i) -> p m i j", i=PACK)
+            copy_on("scalar", dst[:, :SCALAR_COLUMNS], src[:, :SCALAR_COLUMNS])
+            copy_on("vector", dst[:, SCALAR_COLUMNS:], src[:, SCALAR_COLUMNS:])
+            codes = keep.tile([P, SPAN], U32, name="weight_codes_%d_%d_%d" % (a, q, g), align_bytes=64)
+            scales = keep.tile([P, SPAN], U8, name="weight_scales_%d_%d_%d" % (a, q, g), align_bytes=64)
+            quantise(grouped, codes[:], scales[:], products[q][1])
+            weight_mx[a, q, g] = (codes, scales)
+
+        def quantise_moving(q, g):
+            raw = moving_raw[q, g]
+            halves = [
+                interleave(engine, raw[:, :, h * N_TILE : (h + 1) * N_TILE])
+                for h, engine in enumerate(("vector", "scalar"))
+            ]
+            for h in range(COL_HALVES):
+                codes = keep.tile([P, N_TILE], U32, name="moving_codes_%d_%d_%d" % (q, g, h), align_bytes=64)
+                scales = keep.tile([P, N_TILE], U8, name="moving_scales_%d_%d_%d" % (q, g, h), align_bytes=64)
+                quantise(halves[h], codes[:], scales[:], products[q][3])
+                moving_mx[q, g, h] = (codes, scales)
+
+        def multiply(a, q, g):
+            first, last = (q, g) == passes[0], (q, g) == passes[-1]
+            for i in range(PACK):
+                for h in range(COL_HALVES):
+                    if first:
+                        banks[a, i, h] = psum.tile([P, N_TILE], F32, name="bank_%d_%d" % (i, h))
+                    w_codes, w_scales = weight_mx[a, q, g]
+                    m_codes, m_scales = moving_mx[q, g, h]
+                    cols = slice(i * P, (i + 1) * P)
+                    nc.tensor.matmul_mx(
+                        out=banks[a, i, h][:],
+                        lhsT=w_codes[:, cols].bitcast(products[q][1]),
+                        lhsT_scale=w_scales[:, cols],
+                        rhs=m_codes[:].bitcast(products[q][3]),
+                        rhs_scale=m_scales[:],
+                        start=first,
+                        stop=last,
+                    )
+
+        def add_residual(a):
+            for i in range(PACK):
+                for h in range(COL_HALVES):
+                    part = result[a][:, i, h * N_TILE : (h + 1) * N_TILE]
+                    nc.vector.tensor_tensor(out=part, in0=banks[a, i, h][:], in1=part, op=mybir.AluOpType.add)
+
+        out_codes = keep.tile([P, ROW_GROUPS, T], U32, align_bytes=64)
+        out_scales = keep.tile([P, ROW_GROUPS, T], U8, align_bytes=64)
+
+        def quantise_result(a, engines):
+            halves = [
+                interleave(engine, result[a][:, :, h * N_TILE : (h + 1) * N_TILE])
+                for h, engine in enumerate(engines)
+            ]
+            for h in range(COL_HALVES):
+                cols = slice(h * N_TILE, (h + 1) * N_TILE)
+                quantise(halves[h], out_codes[:, a, cols], out_scales[:, a, cols], E4M3)
+
+        for q, g in passes:
+            quantise_weight(0, q, g)
+            quantise_moving(q, g)
+            multiply(0, q, g)
+        add_residual(0)
+        for q, g in passes:
+            quantise_weight(1, q, g)
+            multiply(1, q, g)
+        add_residual(1)
+        quantise_result(0, ("scalar", "scalar"))
+        quantise_result(1, ("vector", "scalar"))
+
+        for a in range(ROW_GROUPS):
+            rows = rows_on_partitions(out_0, a * SPAN)
+            for i0 in range(0, PACK, ROW_PAIR):
+                nc.sync.dma_start(out=rows[:, i0 : i0 + ROW_PAIR, :], in_=result[a][:, i0 : i0 + ROW_PAIR, :])
+
+        def store_codes(a):
+            dram = out_1[a].rearrange("p t i -> p (t i)").bitcast(I32)
+            nc.sync.dma_start(out=dram, in_=out_codes[:, a, :].bitcast(I32))
+
+        store_codes(0)
+        for quadrant in range(4):
+            dram = out_2[:, 4 * quadrant : 4 * quadrant + 4, :].rearrange("a s t -> s a t").bitcast(I32)
+            nc.sync.dma_start(out=dram, in_=out_scales[32 * quadrant : 32 * quadrant + 4].bitcast(I32))
+        store_codes(1)

@@ -22,6 +22,7 @@ ROW_GROUPS = M // SPAN
 COL_HALVES = T // N_TILE
 SCALAR_COLUMNS = 48
 ROW_PAIR = 2
+LEAD = 3
 
 
 def tile_mix_jvp_fm_pl_res_kernel(tc, w, xd, wd, x, r, out_0, out_1, out_2):
@@ -40,11 +41,12 @@ def tile_mix_jvp_fm_pl_res_kernel(tc, w, xd, wd, x, r, out_0, out_1, out_2):
 
         weight_raw, moving_raw, result = {}, {}, {}
 
-        def load_weight(a, q, g):
-            raw = keep.tile([P, PACK, SPAN], F32, name="weight_raw_%d_%d_%d" % (a, q, g))
+        def load_weight(groups, q, g):
+            raw = keep.tile([P, PACK, SPAN * len(groups)], F32, name="weight_raw_%d_%d_%d" % (groups[0], q, g))
             rows = rows_on_partitions(products[q][0], g * SPAN)
-            nc.sync.dma_start(out=raw[:], in_=rows[:, :, a * SPAN : (a + 1) * SPAN])
-            weight_raw[a, q, g] = raw
+            nc.sync.dma_start(out=raw[:], in_=rows[:, :, groups[0] * SPAN : (groups[-1] + 1) * SPAN])
+            for a in groups:
+                weight_raw[a, q, g] = raw[:, :, (a - groups[0]) * SPAN : (a - groups[0] + 1) * SPAN]
 
         def load_moving(q, g):
             raw = keep.tile([P, PACK, T], F32, name="moving_raw_%d_%d" % (q, g))
@@ -58,12 +60,16 @@ def tile_mix_jvp_fm_pl_res_kernel(tc, w, xd, wd, x, r, out_0, out_1, out_2):
                 nc.sync.dma_start(out=res[:, i0 : i0 + ROW_PAIR, :], in_=rows[:, i0 : i0 + ROW_PAIR, :])
             result[a] = res
 
-        for q, g in passes:
-            load_weight(0, q, g)
-            load_moving(q, g)
+        for g in range(K_PASSES):
+            load_weight((0, 1), 0, g)
+            load_moving(0, g)
+        load_weight((0,), 1, 0)
+        load_moving(1, 0)
+        load_moving(1, 1)
+        load_weight((0,), 1, 1)
         load_residual(0)
-        for q, g in passes:
-            load_weight(1, q, g)
+        for g in range(K_PASSES):
+            load_weight((1,), 1, g)
         load_residual(1)
 
         def copy_on(engine, out, in_):
@@ -89,7 +95,7 @@ def tile_mix_jvp_fm_pl_res_kernel(tc, w, xd, wd, x, r, out_0, out_1, out_2):
         def quantise_weight(a, q, g):
             grouped = stage.tile([P, SPAN * PACK], BF16, name="grouped", align_bytes=64)
             dst = grouped[:].rearrange("p (i m j) -> p m i j", i=PACK, j=PACK)
-            src = weight_raw[a, q, g][:].rearrange("p j (m i) -> p m i j", i=PACK)
+            src = weight_raw[a, q, g].rearrange("p j (m i) -> p m i j", i=PACK)
             copy_on("scalar", dst[:, :SCALAR_COLUMNS], src[:, :SCALAR_COLUMNS])
             copy_on("vector", dst[:, SCALAR_COLUMNS:], src[:, SCALAR_COLUMNS:])
             codes = keep.tile([P, SPAN], U32, name="weight_codes_%d_%d_%d" % (a, q, g), align_bytes=64)
@@ -109,24 +115,24 @@ def tile_mix_jvp_fm_pl_res_kernel(tc, w, xd, wd, x, r, out_0, out_1, out_2):
                 quantise(halves[h], codes[:], scales[:], products[q][3])
                 moving_mx[q, g, h] = (codes, scales)
 
-        def multiply(a, q, g):
+        bank_order = [(i, h) for i in range(PACK) for h in range(COL_HALVES)]
+
+        def multiply(a, q, g, i, h):
             first, last = (q, g) == passes[0], (q, g) == passes[-1]
-            for i in range(PACK):
-                for h in range(COL_HALVES):
-                    if first:
-                        banks[a, i, h] = psum.tile([P, N_TILE], F32, name="bank_%d_%d" % (i, h))
-                    w_codes, w_scales = weight_mx[a, q, g]
-                    m_codes, m_scales = moving_mx[q, g, h]
-                    cols = slice(i * P, (i + 1) * P)
-                    nc.tensor.matmul_mx(
-                        out=banks[a, i, h][:],
-                        lhsT=w_codes[:, cols].bitcast(products[q][1]),
-                        lhsT_scale=w_scales[:, cols],
-                        rhs=m_codes[:].bitcast(products[q][3]),
-                        rhs_scale=m_scales[:],
-                        start=first,
-                        stop=last,
-                    )
+            if first:
+                banks[a, i, h] = psum.tile([P, N_TILE], F32, name="bank_%d_%d" % (i, h))
+            w_codes, w_scales = weight_mx[a, q, g]
+            m_codes, m_scales = moving_mx[q, g, h]
+            cols = slice(i * P, (i + 1) * P)
+            nc.tensor.matmul_mx(
+                out=banks[a, i, h][:],
+                lhsT=w_codes[:, cols].bitcast(products[q][1]),
+                lhsT_scale=w_scales[:, cols],
+                rhs=m_codes[:].bitcast(products[q][3]),
+                rhs_scale=m_scales[:],
+                start=first,
+                stop=last,
+            )
 
         def add_residual(a):
             for i in range(PACK):
@@ -146,22 +152,36 @@ def tile_mix_jvp_fm_pl_res_kernel(tc, w, xd, wd, x, r, out_0, out_1, out_2):
                 cols = slice(h * N_TILE, (h + 1) * N_TILE)
                 quantise(halves[h], out_codes[:, a, cols], out_scales[:, a, cols], E4M3)
 
+        for g in range(K_PASSES):
+            quantise_weight(0, 0, g)
+            quantise_weight(1, 0, g)
+            quantise_moving(0, g)
+        quantise_weight(0, 1, 0)
+        quantise_moving(1, 0)
+        quantise_moving(1, 1)
+        quantise_weight(0, 1, 1)
         for q, g in passes:
-            quantise_weight(0, q, g)
-            quantise_moving(q, g)
-            multiply(0, q, g)
+            for i, h in bank_order:
+                multiply(0, q, g, i, h)
         add_residual(0)
-        for q, g in passes:
-            quantise_weight(1, q, g)
-            multiply(1, q, g)
+        for g in range(K_PASSES):
+            quantise_weight(1, 1, g)
+        for i, h in bank_order:
+            for g in range(K_PASSES):
+                multiply(1, 0, g, i, h)
+        for step in range(len(bank_order) + LEAD):
+            if step >= LEAD:
+                multiply(1, 1, 1, *bank_order[step - LEAD])
+            if step < len(bank_order):
+                multiply(1, 1, 0, *bank_order[step])
         add_residual(1)
         quantise_result(0, ("scalar", "scalar"))
         quantise_result(1, ("vector", "scalar"))
 
-        for a in range(ROW_GROUPS):
-            rows = rows_on_partitions(out_0, a * SPAN)
-            for i0 in range(0, PACK, ROW_PAIR):
-                nc.sync.dma_start(out=rows[:, i0 : i0 + ROW_PAIR, :], in_=result[a][:, i0 : i0 + ROW_PAIR, :])
+        nc.sync.dma_start(out=rows_on_partitions(out_0, 0), in_=result[0][:])
+        rows = rows_on_partitions(out_0, SPAN)
+        for i0 in range(0, PACK, ROW_PAIR):
+            nc.sync.dma_start(out=rows[:, i0 : i0 + ROW_PAIR, :], in_=result[1][:, i0 : i0 + ROW_PAIR, :])
 
         def store_codes(a):
             dram = out_1[a].rearrange("p t i -> p (t i)").bitcast(I32)

@@ -17,177 +17,182 @@ P = 128
 PACK = 4
 SPAN = P * PACK
 N_TILE = 512
-K_PASSES = K // SPAN
 ROW_GROUPS = M // SPAN
 COL_HALVES = T // N_TILE
-SCALAR_COLUMNS = 48
-ROW_PAIR = 2
-LEAD = 3
+BANKS = PACK * COL_HALVES
+PAIRS = (slice(0, 2), slice(2, 4))
+RUN = 4
+STAGE_BUFS = 5
 
 
 def tile_mix_jvp_fm_pl_res_kernel(tc, w, xd, wd, x, r, out_0, out_1, out_2):
     nc = tc.nc
-    products = [(w, E4M3, xd, E5M2), (wd, E5M2, x, E4M3)]
-    passes = [(q, g) for q in range(len(products)) for g in range(K_PASSES)]
+    weights = [(w, E4M3), (wd, E5M2)]
+    movings = [(xd, E5M2), (x, E4M3)]
+    passes = [(0, 0), (0, 1), (1, 0), (1, 1)]
 
     with ExitStack() as ctx:
         keep = ctx.enter_context(tc.tile_pool(name="keep", bufs=1))
-        stage = ctx.enter_context(tc.tile_pool(name="stage", bufs=4))
+        stage = ctx.enter_context(tc.tile_pool(name="stage", bufs=STAGE_BUFS))
         psum = ctx.enter_context(tc.psum_pool(name="psum", bufs=1))
         ctx.enter_context(tc.manual_schedule())
 
         def rows_on_partitions(dram, first_row):
             return dram[first_row : first_row + SPAN, :].rearrange("(p j) c -> p j c", j=PACK)
 
-        weight_raw, moving_raw, result = {}, {}, {}
+        def column_half(h):
+            return slice(h * N_TILE, (h + 1) * N_TILE)
 
-        def load_weight(groups, q, g):
-            raw = keep.tile([P, PACK, SPAN * len(groups)], F32, name="weight_raw_%d_%d_%d" % (groups[0], q, g))
-            rows = rows_on_partitions(products[q][0], g * SPAN)
-            nc.sync.dma_start(out=raw[:], in_=rows[:, :, groups[0] * SPAN : (groups[-1] + 1) * SPAN])
-            for a in groups:
-                weight_raw[a, q, g] = raw[:, :, (a - groups[0]) * SPAN : (a - groups[0] + 1) * SPAN]
+        def load_rows(dram, g, name):
+            raw = keep.tile([P, PACK, dram.shape[1]], F32, name=name)
+            nc.sync.dma_start(out=raw[:], in_=rows_on_partitions(dram, g * SPAN))
+            return raw
 
-        def load_moving(q, g):
-            raw = keep.tile([P, PACK, T], F32, name="moving_raw_%d_%d" % (q, g))
-            nc.sync.dma_start(out=raw[:], in_=rows_on_partitions(products[q][2], g * SPAN))
-            moving_raw[q, g] = raw
+        arrival = [
+            ("weight", 0, 0), ("moving", 0, 0), ("weight", 0, 1), ("moving", 0, 1),
+            ("weight", 1, 0), ("moving", 1, 1), ("moving", 1, 0), ("weight", 1, 1),
+        ]
+        raw = {}
+        for side, q, g in arrival:
+            dram = (weights if side == "weight" else movings)[q][0]
+            raw[side, q, g] = load_rows(dram, g, "raw_%s_%d_%d" % (side, q, g))
+        result = {}
+        for a in range(ROW_GROUPS):
+            result[a] = keep.tile([P, PACK, T], F32, name="result_%d" % a)
+            for pair in PAIRS:
+                nc.sync.dma_start(out=result[a][:, pair, :], in_=rows_on_partitions(r, a * SPAN)[:, pair, :])
 
-        def load_residual(a):
-            res = keep.tile([P, PACK, T], F32, name="result_%d" % a)
-            rows = rows_on_partitions(r, a * SPAN)
-            for i0 in range(0, PACK, ROW_PAIR):
-                nc.sync.dma_start(out=res[:, i0 : i0 + ROW_PAIR, :], in_=rows[:, i0 : i0 + ROW_PAIR, :])
-            result[a] = res
+        copy_on = {"vector": nc.vector.tensor_copy, "scalar": nc.scalar.copy}
 
-        for g in range(K_PASSES):
-            load_weight((0, 1), 0, g)
-            load_moving(0, g)
-        load_weight((0,), 1, 0)
-        load_moving(1, 0)
-        load_moving(1, 1)
-        load_weight((0,), 1, 1)
-        load_residual(0)
-        for g in range(K_PASSES):
-            load_weight((1,), 1, g)
-        load_residual(1)
-
-        def copy_on(engine, out, in_):
-            if engine == "vector":
-                nc.vector.tensor_copy(out=out, in_=in_)
-            else:
-                nc.scalar.copy(out=out, in_=in_)
+        def staging_tile():
+            return stage.tile([P, N_TILE * PACK], BF16, name="staged", align_bytes=64)
 
         def interleave(engine, rows):
-            grouped = stage.tile([P, N_TILE * PACK], BF16, name="grouped", align_bytes=64)
-            copy_on(
-                engine,
-                grouped[:].rearrange("p (c u j) -> p c j u", u=4, j=PACK),
-                rows.rearrange("p j (c u) -> p c j u", u=4),
+            staged = staging_tile()
+            copy_on[engine](
+                out=staged[:].rearrange("p (c u j) -> p c j u", u=RUN, j=PACK),
+                in_=rows.rearrange("p j (c u) -> p c j u", u=RUN),
             )
-            return grouped
+            return staged
 
-        def quantise(grouped, codes, scales, fmt):
-            nc.vector.quantize_mx(out=codes.bitcast(fmt), scales=scales, in_=grouped[:])
+        def mx_tiles(name):
+            codes = keep.tile([P, N_TILE], U32, name="codes_" + name, align_bytes=64)
+            scales = keep.tile([P, N_TILE], U8, name="scales_" + name, align_bytes=64)
+            return codes, scales
 
-        weight_mx, moving_mx, banks = {}, {}, {}
+        weight_staged, weight_mx, moving_mx, banks, rounded = {}, {}, {}, {}, {}
 
-        def quantise_weight(a, q, g):
-            grouped = stage.tile([P, SPAN * PACK], BF16, name="grouped", align_bytes=64)
-            dst = grouped[:].rearrange("p (i m j) -> p m i j", i=PACK, j=PACK)
-            src = weight_raw[a, q, g].rearrange("p j (m i) -> p m i j", i=PACK)
-            copy_on("scalar", dst[:, :SCALAR_COLUMNS], src[:, :SCALAR_COLUMNS])
-            copy_on("vector", dst[:, SCALAR_COLUMNS:], src[:, SCALAR_COLUMNS:])
-            codes = keep.tile([P, SPAN], U32, name="weight_codes_%d_%d_%d" % (a, q, g), align_bytes=64)
-            scales = keep.tile([P, SPAN], U8, name="weight_scales_%d_%d_%d" % (a, q, g), align_bytes=64)
-            quantise(grouped, codes[:], scales[:], products[q][1])
-            weight_mx[a, q, g] = (codes, scales)
+        def deal_weight(engine, a, q, g, pair):
+            if (a, q, g) not in weight_staged:
+                weight_staged[a, q, g] = staging_tile()
+                weight_mx[a, q, g] = mx_tiles("weight_%d_%d_%d" % (a, q, g))
+            dst = weight_staged[a, q, g][:].rearrange("p (i m j) -> p m i j", i=PACK, j=PACK)
+            src = raw["weight", q, g][:, :, a * SPAN : (a + 1) * SPAN].rearrange("p j (m i) -> p m i j", i=PACK)
+            copy_on[engine](out=dst[:, :, pair], in_=src[:, :, pair])
+
+        def quantise_weight_pair(a, q, g, pair):
+            codes, scales = weight_mx[a, q, g]
+            cols = slice(pair.start * P, pair.stop * P)
+            nc.vector.quantize_mx(
+                out=codes[:, cols].bitcast(weights[q][1]),
+                scales=scales[:, cols],
+                in_=weight_staged[a, q, g][:, pair.start * SPAN : pair.stop * SPAN],
+            )
+
+        def quantise_weight(q, g):
+            for a in range(ROW_GROUPS):
+                deal_weight("scalar", a, q, g, PAIRS[1])
+            deal_weight("vector", 0, q, g, PAIRS[0])
+            deal_weight("vector", 1, q, g, PAIRS[0])
+            for a in range(ROW_GROUPS):
+                for pair in PAIRS:
+                    quantise_weight_pair(a, q, g, pair)
 
         def quantise_moving(q, g):
-            raw = moving_raw[q, g]
             halves = [
-                interleave(engine, raw[:, :, h * N_TILE : (h + 1) * N_TILE])
+                interleave(engine, raw["moving", q, g][:, :, column_half(h)])
                 for h, engine in enumerate(("vector", "scalar"))
             ]
             for h in range(COL_HALVES):
-                codes = keep.tile([P, N_TILE], U32, name="moving_codes_%d_%d_%d" % (q, g, h), align_bytes=64)
-                scales = keep.tile([P, N_TILE], U8, name="moving_scales_%d_%d_%d" % (q, g, h), align_bytes=64)
-                quantise(halves[h], codes[:], scales[:], products[q][3])
+                codes, scales = mx_tiles("moving_%d_%d_%d" % (q, g, h))
+                nc.vector.quantize_mx(out=codes[:].bitcast(movings[q][1]), scales=scales[:], in_=halves[h][:])
                 moving_mx[q, g, h] = (codes, scales)
 
-        bank_order = [(i, h) for i in range(PACK) for h in range(COL_HALVES)]
-
-        def multiply(a, q, g, i, h):
+        def multiply(a, q, g, bank):
+            i, h = divmod(bank, COL_HALVES)
             first, last = (q, g) == passes[0], (q, g) == passes[-1]
             if first:
-                banks[a, i, h] = psum.tile([P, N_TILE], F32, name="bank_%d_%d" % (i, h))
+                banks[a, bank] = psum.tile([P, N_TILE], F32, name="bank_%d" % bank)
             w_codes, w_scales = weight_mx[a, q, g]
             m_codes, m_scales = moving_mx[q, g, h]
             cols = slice(i * P, (i + 1) * P)
             nc.tensor.matmul_mx(
-                out=banks[a, i, h][:],
-                lhsT=w_codes[:, cols].bitcast(products[q][1]),
+                out=banks[a, bank][:],
+                lhsT=w_codes[:, cols].bitcast(weights[q][1]),
                 lhsT_scale=w_scales[:, cols],
-                rhs=m_codes[:].bitcast(products[q][3]),
+                rhs=m_codes[:].bitcast(movings[q][1]),
                 rhs_scale=m_scales[:],
                 start=first,
                 stop=last,
             )
 
-        def add_residual(a):
-            for i in range(PACK):
-                for h in range(COL_HALVES):
-                    part = result[a][:, i, h * N_TILE : (h + 1) * N_TILE]
-                    nc.vector.tensor_tensor(out=part, in0=banks[a, i, h][:], in1=part, op=mybir.AluOpType.add)
+        def add_residual(a, some_banks):
+            for bank in some_banks:
+                i, h = divmod(bank, COL_HALVES)
+                part = result[a][:, i, column_half(h)]
+                nc.vector.tensor_tensor(out=part, in0=banks[a, bank][:], in1=part, op=mybir.AluOpType.add)
 
         out_codes = keep.tile([P, ROW_GROUPS, T], U32, align_bytes=64)
         out_scales = keep.tile([P, ROW_GROUPS, T], U8, align_bytes=64)
 
-        def quantise_result(a, engines):
-            halves = [
-                interleave(engine, result[a][:, :, h * N_TILE : (h + 1) * N_TILE])
-                for h, engine in enumerate(engines)
-            ]
+        def round_result(engine, a, h):
+            rounded[a, h] = interleave(engine, result[a][:, :, column_half(h)])
+
+        def quantise_result(a, h):
+            nc.vector.quantize_mx(
+                out=out_codes[:, a, column_half(h)].bitcast(E4M3),
+                scales=out_scales[:, a, column_half(h)],
+                in_=rounded[a, h][:],
+            )
+
+        for side, q, g in arrival:
+            (quantise_weight if side == "weight" else quantise_moving)(q, g)
+
+        for q, g in passes[:-1]:
             for h in range(COL_HALVES):
-                cols = slice(h * N_TILE, (h + 1) * N_TILE)
-                quantise(halves[h], out_codes[:, a, cols], out_scales[:, a, cols], E4M3)
+                for i in range(PACK):
+                    multiply(0, q, g, i * COL_HALVES + h)
+        for bank in range(BANKS):
+            multiply(0, *passes[-1], bank)
+        add_residual(0, range(BANKS))
+        for bank in range(BANKS):
+            for q, g in passes:
+                multiply(1, q, g, bank)
 
-        for g in range(K_PASSES):
-            quantise_weight(0, 0, g)
-            quantise_weight(1, 0, g)
-            quantise_moving(0, g)
-        quantise_weight(0, 1, 0)
-        quantise_moving(1, 0)
-        quantise_moving(1, 1)
-        quantise_weight(0, 1, 1)
-        for q, g in passes:
-            for i, h in bank_order:
-                multiply(0, q, g, i, h)
-        add_residual(0)
-        for g in range(K_PASSES):
-            quantise_weight(1, 1, g)
-        for i, h in bank_order:
-            for g in range(K_PASSES):
-                multiply(1, 0, g, i, h)
-        for step in range(len(bank_order) + LEAD):
-            if step >= LEAD:
-                multiply(1, 1, 1, *bank_order[step - LEAD])
-            if step < len(bank_order):
-                multiply(1, 1, 0, *bank_order[step])
-        add_residual(1)
-        quantise_result(0, ("scalar", "scalar"))
-        quantise_result(1, ("vector", "scalar"))
+        round_result("scalar", 0, 0)
+        round_result("scalar", 0, 1)
+        add_residual(1, range(0, 4))
+        quantise_result(0, 0)
+        add_residual(1, range(4, 7))
+        round_result("scalar", 1, 0)
+        quantise_result(0, 1)
+        add_residual(1, range(7, 8))
+        round_result("vector", 1, 1)
+        quantise_result(1, 0)
+        quantise_result(1, 1)
 
-        nc.sync.dma_start(out=rows_on_partitions(out_0, 0), in_=result[0][:])
-        rows = rows_on_partitions(out_0, SPAN)
-        for i0 in range(0, PACK, ROW_PAIR):
-            nc.sync.dma_start(out=rows[:, i0 : i0 + ROW_PAIR, :], in_=result[1][:, i0 : i0 + ROW_PAIR, :])
+        def store_result(a, pair):
+            nc.sync.dma_start(out=rows_on_partitions(out_0, a * SPAN)[:, pair, :], in_=result[a][:, pair, :])
 
         def store_codes(a):
             dram = out_1[a].rearrange("p t i -> p (t i)").bitcast(I32)
             nc.sync.dma_start(out=dram, in_=out_codes[:, a, :].bitcast(I32))
 
+        store_result(0, PAIRS[0])
+        store_result(0, PAIRS[1])
+        store_result(1, PAIRS[0])
         store_codes(0)
+        store_result(1, PAIRS[1])
         for quadrant in range(4):
             dram = out_2[:, 4 * quadrant : 4 * quadrant + 4, :].rearrange("a s t -> s a t").bitcast(I32)
             nc.sync.dma_start(out=dram, in_=out_scales[32 * quadrant : 32 * quadrant + 4].bitcast(I32))

@@ -67,13 +67,10 @@ def tile_mix_jvp_fm_pl_res_kernel(tc, w, xd, wd, x, r, out_0, out_1, out_2):
         def staging_tile():
             return stage.tile([P, N_TILE * PACK], BF16, name="staged", align_bytes=64)
 
-        def interleave(engine, rows):
-            staged = staging_tile()
-            copy_on[engine](
-                out=staged[:].rearrange("p (c u j) -> p c j u", u=RUN, j=PACK),
-                in_=rows.rearrange("p j (c u) -> p c j u", u=RUN),
-            )
-            return staged
+        def interleave(engine, staged, rows):
+            dst = staged[:].rearrange("p (c u j) -> p c j u", u=RUN, j=PACK)
+            src = rows.rearrange("p j (c u) -> p c j u", u=RUN)
+            copy_on[engine](out=dst, in_=src)
 
         def mx_tiles(name):
             codes = keep.tile([P, N_TILE], U32, name="codes_" + name, align_bytes=64)
@@ -99,27 +96,25 @@ def tile_mix_jvp_fm_pl_res_kernel(tc, w, xd, wd, x, r, out_0, out_1, out_2):
                 in_=weight_staged[a, q, g][:, pair.start * SPAN : pair.stop * SPAN],
             )
 
-        def quantise_weight(q, g):
-            for a in range(ROW_GROUPS):
-                deal_weight("scalar", a, q, g, PAIRS[1])
-            deal_weight("vector", 0, q, g, PAIRS[0])
-            deal_weight("vector", 1, q, g, PAIRS[0])
-            for a in range(ROW_GROUPS):
-                for pair in PAIRS:
-                    quantise_weight_pair(a, q, g, pair)
+        def quantise_weight(a, q, g):
+            deal_weight("vector", a, q, g, PAIRS[0])
+            deal_weight("scalar", a, q, g, PAIRS[1])
+            for pair in PAIRS:
+                quantise_weight_pair(a, q, g, pair)
 
         def quantise_moving(q, g):
-            halves = [
-                interleave(engine, raw["moving", q, g][:, :, column_half(h)])
-                for h, engine in enumerate(("vector", "scalar"))
-            ]
+            halves = [staging_tile() for h in range(COL_HALVES)]
+            for h, engine in enumerate(("vector", "scalar")):
+                interleave(engine, halves[h], raw["moving", q, g][:, :, column_half(h)])
             for h in range(COL_HALVES):
                 codes, scales = mx_tiles("moving_%d_%d_%d" % (q, g, h))
                 nc.vector.quantize_mx(out=codes[:].bitcast(movings[q][1]), scales=scales[:], in_=halves[h][:])
                 moving_mx[q, g, h] = (codes, scales)
 
+        bank_tiles = [(i, h) for i in range(PACK) for h in range(COL_HALVES)]
+
         def multiply(a, q, g, bank):
-            i, h = divmod(bank, COL_HALVES)
+            i, h = bank_tiles[bank]
             first, last = (q, g) == passes[0], (q, g) == passes[-1]
             if first:
                 banks[a, bank] = psum.tile([P, N_TILE], F32, name="bank_%d" % bank)
@@ -138,7 +133,7 @@ def tile_mix_jvp_fm_pl_res_kernel(tc, w, xd, wd, x, r, out_0, out_1, out_2):
 
         def add_residual(a, some_banks):
             for bank in some_banks:
-                i, h = divmod(bank, COL_HALVES)
+                i, h = bank_tiles[bank]
                 part = result[a][:, i, column_half(h)]
                 nc.vector.tensor_tensor(out=part, in0=banks[a, bank][:], in1=part, op=mybir.AluOpType.add)
 
@@ -146,7 +141,8 @@ def tile_mix_jvp_fm_pl_res_kernel(tc, w, xd, wd, x, r, out_0, out_1, out_2):
         out_scales = keep.tile([P, ROW_GROUPS, T], U8, align_bytes=64)
 
         def round_result(engine, a, h):
-            rounded[a, h] = interleave(engine, result[a][:, :, column_half(h)])
+            rounded[a, h] = staging_tile()
+            interleave(engine, rounded[a, h], result[a][:, :, column_half(h)])
 
         def quantise_result(a, h):
             nc.vector.quantize_mx(
@@ -155,25 +151,37 @@ def tile_mix_jvp_fm_pl_res_kernel(tc, w, xd, wd, x, r, out_0, out_1, out_2):
                 in_=rounded[a, h][:],
             )
 
-        for side, q, g in arrival:
-            (quantise_weight if side == "weight" else quantise_moving)(q, g)
+        for side, q, g in arrival[:-1]:
+            if side == "moving":
+                quantise_moving(q, g)
+            else:
+                for a in range(ROW_GROUPS):
+                    quantise_weight(a, q, g)
+        last_pass = passes[-1]
+        quantise_weight(0, *last_pass)
+        for pair in PAIRS:
+            deal_weight("scalar", 1, *last_pass, pair)
 
         for q, g in passes[:-1]:
-            for h in range(COL_HALVES):
-                for i in range(PACK):
-                    multiply(0, q, g, i * COL_HALVES + h)
+            for bank in sorted(range(BANKS), key=lambda b: bank_tiles[b][1]):
+                multiply(0, q, g, bank)
         for bank in range(BANKS):
-            multiply(0, *passes[-1], bank)
-        add_residual(0, range(BANKS))
+            multiply(0, *last_pass, bank)
+
+        add_residual(0, range(0, 1))
+        quantise_weight_pair(1, *last_pass, PAIRS[0])
+        add_residual(0, range(1, 7))
+        round_result("scalar", 0, 0)
+        add_residual(0, range(7, 8))
+        round_result("scalar", 0, 1)
+        quantise_weight_pair(1, *last_pass, PAIRS[1])
         for bank in range(BANKS):
             for q, g in passes:
                 multiply(1, q, g, bank)
 
-        round_result("scalar", 0, 0)
-        round_result("scalar", 0, 1)
-        add_residual(1, range(0, 4))
+        add_residual(1, range(0, 3))
         quantise_result(0, 0)
-        add_residual(1, range(4, 7))
+        add_residual(1, range(3, 7))
         round_result("scalar", 1, 0)
         quantise_result(0, 1)
         add_residual(1, range(7, 8))
@@ -184,16 +192,21 @@ def tile_mix_jvp_fm_pl_res_kernel(tc, w, xd, wd, x, r, out_0, out_1, out_2):
         def store_result(a, pair):
             nc.sync.dma_start(out=rows_on_partitions(out_0, a * SPAN)[:, pair, :], in_=result[a][:, pair, :])
 
-        def store_codes(a):
+        def store_codes(a, cols):
             dram = out_1[a].rearrange("p t i -> p (t i)").bitcast(I32)
-            nc.sync.dma_start(out=dram, in_=out_codes[:, a, :].bitcast(I32))
+            nc.sync.dma_start(out=dram[:, cols], in_=out_codes[:, a, cols].bitcast(I32))
+
+        def store_scales(a):
+            for quadrant in range(4):
+                dram = out_2[a, 4 * quadrant : 4 * quadrant + 4, :].bitcast(I32)
+                nc.sync.dma_start(out=dram, in_=out_scales[32 * quadrant : 32 * quadrant + 4, a, :].bitcast(I32))
 
         store_result(0, PAIRS[0])
         store_result(0, PAIRS[1])
         store_result(1, PAIRS[0])
-        store_codes(0)
+        store_codes(0, slice(0, T))
+        store_scales(0)
         store_result(1, PAIRS[1])
-        for quadrant in range(4):
-            dram = out_2[:, 4 * quadrant : 4 * quadrant + 4, :].rearrange("a s t -> s a t").bitcast(I32)
-            nc.sync.dma_start(out=dram, in_=out_scales[32 * quadrant : 32 * quadrant + 4].bitcast(I32))
-        store_codes(1)
+        for h in range(COL_HALVES):
+            store_codes(1, column_half(h))
+        store_scales(1)

@@ -23,6 +23,7 @@ BANKS = PACK * COL_HALVES
 PAIRS = (slice(0, 2), slice(2, 4))
 RUN = 4
 STAGE_BUFS = 5
+DMA_ALIGN = 256
 
 
 def tile_mix_jvp_fm_pl_res_kernel(tc, w, xd, wd, x, r, out_0, out_1, out_2):
@@ -44,7 +45,7 @@ def tile_mix_jvp_fm_pl_res_kernel(tc, w, xd, wd, x, r, out_0, out_1, out_2):
             return slice(h * N_TILE, (h + 1) * N_TILE)
 
         def load_rows(dram, g, name):
-            raw = keep.tile([P, PACK, dram.shape[1]], F32, name=name)
+            raw = keep.tile([P, PACK, dram.shape[1]], F32, name=name, align_bytes=DMA_ALIGN)
             nc.sync.dma_start(out=raw[:], in_=rows_on_partitions(dram, g * SPAN))
             return raw
 
@@ -58,7 +59,7 @@ def tile_mix_jvp_fm_pl_res_kernel(tc, w, xd, wd, x, r, out_0, out_1, out_2):
             raw[side, q, g] = load_rows(dram, g, "raw_%s_%d_%d" % (side, q, g))
         result = {}
         for a in range(ROW_GROUPS):
-            result[a] = keep.tile([P, PACK, T], F32, name="result_%d" % a)
+            result[a] = keep.tile([P, PACK, T], F32, name="result_%d" % a, align_bytes=DMA_ALIGN)
             for pair in PAIRS:
                 nc.sync.dma_start(out=result[a][:, pair, :], in_=rows_on_partitions(r, a * SPAN)[:, pair, :])
 
@@ -137,8 +138,8 @@ def tile_mix_jvp_fm_pl_res_kernel(tc, w, xd, wd, x, r, out_0, out_1, out_2):
                 part = result[a][:, i, column_half(h)]
                 nc.vector.tensor_tensor(out=part, in0=banks[a, bank][:], in1=part, op=mybir.AluOpType.add)
 
-        out_codes = keep.tile([P, ROW_GROUPS, T], U32, align_bytes=64)
-        out_scales = keep.tile([P, ROW_GROUPS, T], U8, align_bytes=64)
+        out_codes = keep.tile([P, ROW_GROUPS, T], U32, align_bytes=DMA_ALIGN)
+        out_scales = keep.tile([P, ROW_GROUPS, T], U8, align_bytes=DMA_ALIGN)
 
         def round_result(engine, a, h):
             rounded[a, h] = staging_tile()

@@ -180,9 +180,9 @@ def tile_mix_jvp_fm_pl_res_kernel(tc, w, xd, wd, x, r, out_0, out_1, out_2):
             for q, g in passes:
                 multiply(1, q, g, bank)
 
-        add_residual(1, range(0, 3))
+        add_residual(1, range(0, 4))
         quantise_result(0, 0)
-        add_residual(1, range(3, 7))
+        add_residual(1, range(4, 7))
         round_result("scalar", 1, 0)
         quantise_result(0, 1)
         add_residual(1, range(7, 8))
@@ -205,9 +205,10 @@ def tile_mix_jvp_fm_pl_res_kernel(tc, w, xd, wd, x, r, out_0, out_1, out_2):
         store_result(0, PAIRS[0])
         store_result(0, PAIRS[1])
         store_result(1, PAIRS[0])
+        store_result(1, slice(2, 3))
         store_codes(0, slice(0, T))
         store_scales(0)
-        store_result(1, PAIRS[1])
+        store_result(1, slice(3, 4))
         for h in range(COL_HALVES):
             store_codes(1, column_half(h))
         store_scales(1)

@@ -50,8 +50,8 @@ def tile_mix_jvp_fm_pl_res_kernel(tc, w, xd, wd, x, r, out_0, out_1, out_2):
             return raw
 
         arrival = [
-            ("weight", 0, 0), ("moving", 0, 0), ("weight", 0, 1), ("moving", 0, 1),
-            ("weight", 1, 0), ("moving", 1, 1), ("moving", 1, 0), ("weight", 1, 1),
+            ("weight", 0, 0), ("moving", 0, 0), ("weight", 0, 1), ("weight", 1, 0),
+            ("moving", 1, 1), ("moving", 0, 1), ("moving", 1, 0), ("weight", 1, 1),
         ]
         raw = {}
         for side, q, g in arrival:
@@ -145,6 +145,13 @@ def tile_mix_jvp_fm_pl_res_kernel(tc, w, xd, wd, x, r, out_0, out_1, out_2):
             rounded[a, h] = staging_tile()
             interleave(engine, rounded[a, h], result[a][:, :, column_half(h)])
 
+        def round_result_pair(a, h, pair):
+            if (a, h) not in rounded:
+                rounded[a, h] = staging_tile()
+            dst = rounded[a, h][:].rearrange("p (c j) -> p c j", j=PACK)
+            src = result[a][:, pair, column_half(h)].rearrange("p j c -> p c j")
+            nc.scalar.copy(out=dst[:, :, pair], in_=src)
+
         def quantise_result(a, h):
             nc.vector.quantize_mx(
                 out=out_codes[:, a, column_half(h)].bitcast(E4M3),
@@ -169,22 +176,32 @@ def tile_mix_jvp_fm_pl_res_kernel(tc, w, xd, wd, x, r, out_0, out_1, out_2):
         for bank in range(BANKS):
             multiply(0, *last_pass, bank)
 
-        add_residual(0, range(0, 1))
+        add_residual(0, range(0, 3))
+        round_result_pair(0, 0, PAIRS[0])
+        add_residual(0, range(3, 7))
+        round_result_pair(0, 0, PAIRS[1])
         quantise_weight_pair(1, *last_pass, PAIRS[0])
-        add_residual(0, range(1, 7))
-        round_result("scalar", 0, 0)
         add_residual(0, range(7, 8))
         round_result("scalar", 0, 1)
         quantise_weight_pair(1, *last_pass, PAIRS[1])
-        for bank in range(BANKS):
+        first_banks = range(0, BANKS // 2)
+        for bank in first_banks:
+            for q, g in passes[:-1]:
+                multiply(1, q, g, bank)
+        for bank in first_banks:
+            multiply(1, *last_pass, bank)
+        for bank in range(BANKS // 2, BANKS):
             for q, g in passes:
                 multiply(1, q, g, bank)
 
-        add_residual(1, range(0, 4))
+        add_residual(1, range(0, 3))
+        round_result_pair(1, 0, PAIRS[0])
+        add_residual(1, range(3, 4))
         quantise_result(0, 0)
-        add_residual(1, range(4, 7))
-        round_result("scalar", 1, 0)
+        add_residual(1, range(4, 5))
         quantise_result(0, 1)
+        add_residual(1, range(5, 7))
+        round_result_pair(1, 0, PAIRS[1])
         add_residual(1, range(7, 8))
         round_result("vector", 1, 1)
         quantise_result(1, 0)
@@ -205,10 +222,8 @@ def tile_mix_jvp_fm_pl_res_kernel(tc, w, xd, wd, x, r, out_0, out_1, out_2):
         store_result(0, PAIRS[0])
         store_result(0, PAIRS[1])
         store_result(1, PAIRS[0])
-        store_result(1, slice(2, 3))
         store_codes(0, slice(0, T))
         store_scales(0)
-        store_result(1, slice(3, 4))
-        for h in range(COL_HALVES):
-            store_codes(1, column_half(h))
+        store_result(1, PAIRS[1])
+        store_codes(1, slice(0, T))
         store_scales(1)

@@ -30,7 +30,7 @@ def tile_mix_jvp_fm_pl_res_kernel(tc, w, xd, wd, x, r, out_0, out_1, out_2):
     nc = tc.nc
     weights = [(w, E4M3), (wd, E5M2)]
     movings = [(xd, E5M2), (x, E4M3)]
-    passes = [(0, 0), (0, 1), (1, 0), (1, 1)]
+    passes = [(1, 0), (0, 0), (0, 1), (1, 1)]
 
     with ExitStack() as ctx:
         keep = ctx.enter_context(tc.tile_pool(name="keep", bufs=1))
@@ -44,19 +44,27 @@ def tile_mix_jvp_fm_pl_res_kernel(tc, w, xd, wd, x, r, out_0, out_1, out_2):
         def column_half(h):
             return slice(h * N_TILE, (h + 1) * N_TILE)
 
-        def load_rows(dram, g, name):
-            raw = keep.tile([P, PACK, dram.shape[1]], F32, name=name, align_bytes=DMA_ALIGN)
-            nc.sync.dma_start(out=raw[:], in_=rows_on_partitions(dram, g * SPAN))
-            return raw
+        def load_passes(dram, some_passes, name):
+            n = len(some_passes)
+            rows = dram[some_passes.start * SPAN : some_passes.stop * SPAN, :]
+            tile_raw = keep.tile([P, n, PACK, dram.shape[1]], F32, name=name, align_bytes=DMA_ALIGN)
+            nc.sync.dma_start(
+                out=tile_raw[:].rearrange("p g j c -> p g (j c)"),
+                in_=rows.rearrange("(g p j) c -> p g (j c)", p=P, j=PACK),
+            )
+            return tile_raw
 
-        arrival = [
-            ("weight", 0, 0), ("moving", 0, 0), ("weight", 0, 1), ("weight", 1, 0),
-            ("moving", 1, 1), ("moving", 0, 1), ("moving", 1, 0), ("weight", 1, 1),
+        loads = [
+            ("weight", 0, range(0, 2)), ("moving", 1, range(0, 2)), ("weight", 1, range(0, 1)),
+            ("moving", 0, range(0, 1)), ("moving", 0, range(1, 2)), ("weight", 1, range(1, 2)),
         ]
-        raw = {}
-        for side, q, g in arrival:
+        raw, arrival = {}, []
+        for side, q, some_passes in loads:
             dram = (weights if side == "weight" else movings)[q][0]
-            raw[side, q, g] = load_rows(dram, g, "raw_%s_%d_%d" % (side, q, g))
+            loaded = load_passes(dram, some_passes, "raw_%s_%d_%d" % (side, q, some_passes.start))
+            for g in some_passes:
+                raw[side, q, g] = loaded[:, g - some_passes.start]
+                arrival.append((side, q, g))
         result = {}
         for a in range(ROW_GROUPS):
             result[a] = keep.tile([P, PACK, T], F32, name="result_%d" % a, align_bytes=DMA_ALIGN)

@@ -71,7 +71,12 @@ def tile_mix_jvp_fm_pl_res_kernel(tc, w, xd, wd, x, r, out_0, out_1, out_2):
             for pair in PAIRS:
                 nc.sync.dma_start(out=result[a][:, pair, :], in_=rows_on_partitions(r, a * SPAN)[:, pair, :])
 
-        copy_on = {"vector": nc.vector.tensor_copy, "scalar": nc.scalar.copy}
+        def gpsimd_copy(out, in_):
+            nc.gpsimd.tensor_scalar(
+                out=out, in0=in_, scalar1=1.0, scalar2=-0.0, op0=mybir.AluOpType.mult, op1=mybir.AluOpType.add
+            )
+
+        copy_on = {"vector": nc.vector.tensor_copy, "scalar": nc.scalar.copy, "gpsimd": gpsimd_copy}
 
         def staging_tile():
             return stage.tile([P, N_TILE * PACK], BF16, name="staged", align_bytes=64)
@@ -153,12 +158,12 @@ def tile_mix_jvp_fm_pl_res_kernel(tc, w, xd, wd, x, r, out_0, out_1, out_2):
             rounded[a, h] = staging_tile()
             interleave(engine, rounded[a, h], result[a][:, :, column_half(h)])
 
-        def round_result_pair(a, h, pair):
+        def round_result_pair(engine, a, h, pair):
             if (a, h) not in rounded:
                 rounded[a, h] = staging_tile()
             dst = rounded[a, h][:].rearrange("p (c j) -> p c j", j=PACK)
             src = result[a][:, pair, column_half(h)].rearrange("p j c -> p c j")
-            nc.scalar.copy(out=dst[:, :, pair], in_=src)
+            copy_on[engine](out=dst[:, :, pair], in_=src)
 
         def quantise_result(a, h):
             nc.vector.quantize_mx(
@@ -185,13 +190,12 @@ def tile_mix_jvp_fm_pl_res_kernel(tc, w, xd, wd, x, r, out_0, out_1, out_2):
             multiply(0, *last_pass, bank)
 
         add_residual(0, range(0, 3))
-        round_result_pair(0, 0, PAIRS[0])
+        round_result_pair("scalar", 0, 0, PAIRS[0])
         add_residual(0, range(3, 7))
-        round_result_pair(0, 0, PAIRS[1])
-        quantise_weight_pair(1, *last_pass, PAIRS[0])
+        round_result_pair("scalar", 0, 0, PAIRS[1])
+        quantise_weight_pair(1, *last_pass, slice(0, PACK))
         add_residual(0, range(7, 8))
-        round_result("scalar", 0, 1)
-        quantise_weight_pair(1, *last_pass, PAIRS[1])
+        round_result("gpsimd", 0, 1)
         first_banks = range(0, BANKS // 2)
         for bank in first_banks:
             for q, g in passes[:-1]:
@@ -203,15 +207,16 @@ def tile_mix_jvp_fm_pl_res_kernel(tc, w, xd, wd, x, r, out_0, out_1, out_2):
                 multiply(1, q, g, bank)
 
         add_residual(1, range(0, 3))
-        round_result_pair(1, 0, PAIRS[0])
+        round_result_pair("scalar", 1, 0, PAIRS[0])
         add_residual(1, range(3, 4))
-        quantise_result(0, 0)
+        round_result_pair("scalar", 1, 1, PAIRS[0])
         add_residual(1, range(4, 5))
+        quantise_result(0, 0)
         quantise_result(0, 1)
         add_residual(1, range(5, 7))
-        round_result_pair(1, 0, PAIRS[1])
+        round_result_pair("scalar", 1, 0, PAIRS[1])
         add_residual(1, range(7, 8))
-        round_result("vector", 1, 1)
+        round_result_pair("vector", 1, 1, PAIRS[1])
         quantise_result(1, 0)
         quantise_result(1, 1)
 

@@ -227,16 +227,15 @@ def tile_mix_jvp_fm_pl_res_kernel(tc, w, xd, wd, x, r, out_0, out_1, out_2):
             dram = out_1[a].rearrange("p t i -> p (t i)").bitcast(I32)
             nc.sync.dma_start(out=dram[:, cols], in_=out_codes[:, a, cols].bitcast(I32))
 
-        def store_scales(a):
-            for quadrant in range(4):
-                dram = out_2[a, 4 * quadrant : 4 * quadrant + 4, :].bitcast(I32)
-                nc.sync.dma_start(out=dram, in_=out_scales[32 * quadrant : 32 * quadrant + 4, a, :].bitcast(I32))
+        def store_scales():
+            for row in range(4):
+                dram = out_2[:, row::4, :].rearrange("a q t -> q a t").bitcast(I32)
+                nc.sync.dma_start(out=dram, in_=out_scales[row:P:32].bitcast(I32))
 
         store_result(0, PAIRS[0])
         store_result(0, PAIRS[1])
         store_result(1, PAIRS[0])
         store_codes(0, slice(0, T))
-        store_scales(0)
         store_result(1, PAIRS[1])
         store_codes(1, slice(0, T))
-        store_scales(1)
+        store_scales()

@@ -127,9 +127,9 @@ def tile_mix_jvp_fm_pl_res_kernel(tc, w, xd, wd, x, r, out_0, out_1, out_2):
 
         bank_tiles = [(i, h) for i in range(PACK) for h in range(COL_HALVES)]
 
-        def multiply(a, q, g, bank):
+        def multiply(a, q, g, bank, closing=passes[-1]):
             i, h = bank_tiles[bank]
-            first, last = (q, g) == passes[0], (q, g) == passes[-1]
+            first, last = (q, g) == passes[0], (q, g) == closing
             if first:
                 banks[a, bank] = psum.tile([P, N_TILE], F32, name="bank_%d" % bank)
             w_codes, w_scales = weight_mx[a, q, g]
@@ -184,7 +184,7 @@ def tile_mix_jvp_fm_pl_res_kernel(tc, w, xd, wd, x, r, out_0, out_1, out_2):
             deal_weight("scalar", 1, *last_pass, pair)
 
         for q, g in passes[:-1]:
-            for bank in sorted(range(BANKS), key=lambda b: bank_tiles[b][1]):
+            for bank in range(BANKS):
                 multiply(0, q, g, bank)
         for bank in range(BANKS):
             multiply(0, *last_pass, bank)
@@ -197,14 +197,20 @@ def tile_mix_jvp_fm_pl_res_kernel(tc, w, xd, wd, x, r, out_0, out_1, out_2):
         add_residual(0, range(7, 8))
         round_result("gpsimd", 0, 1)
         first_banks = range(0, BANKS // 2)
-        for bank in first_banks:
+        for left in first_banks[::COL_HALVES]:
             for q, g in passes[:-1]:
-                multiply(1, q, g, bank)
+                multiply(1, q, g, left)
+                multiply(1, q, g, left + 1)
         for bank in first_banks:
             multiply(1, *last_pass, bank)
-        for bank in range(BANKS // 2, BANKS):
-            for q, g in passes:
-                multiply(1, q, g, bank)
+        for left in range(BANKS // 2, BANKS, COL_HALVES):
+            for q, g in passes[:2]:
+                multiply(1, q, g, left)
+                multiply(1, q, g, left + 1)
+            multiply(1, *passes[2], left)
+            multiply(1, *passes[3], left)
+            multiply(1, *passes[3], left + 1, closing=passes[2])
+            multiply(1, *passes[2], left + 1, closing=passes[2])
 
         add_residual(1, range(0, 3))
         round_result_pair("scalar", 1, 0, PAIRS[0])

from contextlib import ExitStack

import concourse.mybir as mybir

K, M, T = 1024, 1024, 1024
FLOPS = 2 * 2 * K * M * T

F32 = mybir.dt.float32
BF16 = mybir.dt.bfloat16
U32 = mybir.dt.uint32
I32 = mybir.dt.int32
U8 = mybir.dt.uint8
E4M3 = mybir.dt.float8_e4m3fn_x4
E5M2 = mybir.dt.float8_e5m2_x4

P = 128
PACK = 4
SPAN = P * PACK
N_TILE = 512
ROW_GROUPS = M // SPAN
COL_HALVES = T // N_TILE
BANKS = PACK * COL_HALVES
PAIRS = (slice(0, 2), slice(2, 4))
RUN = 4
STAGE_BUFS = 5
DMA_ALIGN = 256


def tile_mix_jvp_fm_pl_res_kernel(tc, w, xd, wd, x, r, out_0, out_1, out_2):
    nc = tc.nc
    weights = [(w, E4M3), (wd, E5M2)]
    movings = [(xd, E5M2), (x, E4M3)]
    passes = [(1, 0), (0, 0), (0, 1), (1, 1)]

    with ExitStack() as ctx:
        keep = ctx.enter_context(tc.tile_pool(name="keep", bufs=1))
        stage = ctx.enter_context(tc.tile_pool(name="stage", bufs=STAGE_BUFS))
        psum = ctx.enter_context(tc.psum_pool(name="psum", bufs=1))
        ctx.enter_context(tc.manual_schedule())

        def rows_on_partitions(dram, first_row):
            return dram[first_row : first_row + SPAN, :].rearrange("(p j) c -> p j c", j=PACK)

        def column_half(h):
            return slice(h * N_TILE, (h + 1) * N_TILE)

        def load_passes(dram, some_passes, name):
            n = len(some_passes)
            rows = dram[some_passes.start * SPAN : some_passes.stop * SPAN, :]
            tile_raw = keep.tile([P, n, PACK, dram.shape[1]], F32, name=name, align_bytes=DMA_ALIGN)
            nc.sync.dma_start(
                out=tile_raw[:].rearrange("p g j c -> p g (j c)"),
                in_=rows.rearrange("(g p j) c -> p g (j c)", p=P, j=PACK),
            )
            return tile_raw

        loads = [
            ("weight", 0, range(0, 2)), ("moving", 1, range(0, 2)), ("weight", 1, range(0, 1)),
            ("moving", 0, range(0, 1)), ("moving", 0, range(1, 2)), ("weight", 1, range(1, 2)),
        ]
        raw, arrival = {}, []
        for side, q, some_passes in loads:
            dram = (weights if side == "weight" else movings)[q][0]
            loaded = load_passes(dram, some_passes, "raw_%s_%d_%d" % (side, q, some_passes.start))
            for g in some_passes:
                raw[side, q, g] = loaded[:, g - some_passes.start]
                arrival.append((side, q, g))
        result = {}
        for a in range(ROW_GROUPS):
            result[a] = keep.tile([P, PACK, T], F32, name="result_%d" % a, align_bytes=DMA_ALIGN)
            for pair in PAIRS:
                nc.sync.dma_start(out=result[a][:, pair, :], in_=rows_on_partitions(r, a * SPAN)[:, pair, :])

        def gpsimd_copy(out, in_):
            nc.gpsimd.tensor_scalar(
                out=out, in0=in_, scalar1=1.0, scalar2=-0.0, op0=mybir.AluOpType.mult, op1=mybir.AluOpType.add
            )

        copy_on = {"vector": nc.vector.tensor_copy, "scalar": nc.scalar.copy, "gpsimd": gpsimd_copy}

        def staging_tile():
            return stage.tile([P, N_TILE * PACK], BF16, name="staged", align_bytes=64)

        def interleave(engine, staged, rows):
            dst = staged[:].rearrange("p (c u j) -> p c j u", u=RUN, j=PACK)
            src = rows.rearrange("p j (c u) -> p c j u", u=RUN)
            copy_on[engine](out=dst, in_=src)

        def mx_tiles(name):
            codes = keep.tile([P, N_TILE], U32, name="codes_" + name, align_bytes=64)
            scales = keep.tile([P, N_TILE], U8, name="scales_" + name, align_bytes=64)
            return codes, scales

        weight_staged, weight_mx, moving_mx, banks, rounded = {}, {}, {}, {}, {}

        def deal_weight(engine, a, q, g, pair):
            if (a, q, g) not in weight_staged:
                weight_staged[a, q, g] = staging_tile()
                weight_mx[a, q, g] = mx_tiles("weight_%d_%d_%d" % (a, q, g))
            dst = weight_staged[a, q, g][:].rearrange("p (i m j) -> p m i j", i=PACK, j=PACK)
            src = raw["weight", q, g][:, :, a * SPAN : (a + 1) * SPAN].rearrange("p j (m i) -> p m i j", i=PACK)
            copy_on[engine](out=dst[:, :, pair], in_=src[:, :, pair])

        def quantise_weight_pair(a, q, g, pair):
            codes, scales = weight_mx[a, q, g]
            cols = slice(pair.start * P, pair.stop * P)
            nc.vector.quantize_mx(
                out=codes[:, cols].bitcast(weights[q][1]),
                scales=scales[:, cols],
                in_=weight_staged[a, q, g][:, pair.start * SPAN : pair.stop * SPAN],
            )

        def quantise_weight(a, q, g):
            deal_weight("vector", a, q, g, PAIRS[0])
            deal_weight("scalar", a, q, g, PAIRS[1])
            for pair in PAIRS:
                quantise_weight_pair(a, q, g, pair)

        def quantise_moving(q, g):
            halves = [staging_tile() for h in range(COL_HALVES)]
            for h, engine in enumerate(("vector", "scalar")):
                interleave(engine, halves[h], raw["moving", q, g][:, :, column_half(h)])
            for h in range(COL_HALVES):
                codes, scales = mx_tiles("moving_%d_%d_%d" % (q, g, h))
                nc.vector.quantize_mx(out=codes[:].bitcast(movings[q][1]), scales=scales[:], in_=halves[h][:])
                moving_mx[q, g, h] = (codes, scales)

        bank_tiles = [(i, h) for i in range(PACK) for h in range(COL_HALVES)]

        def multiply(a, q, g, bank, closing=passes[-1]):
            i, h = bank_tiles[bank]
            first, last = (q, g) == passes[0], (q, g) == closing
            if first:
                banks[a, bank] = psum.tile([P, N_TILE], F32, name="bank_%d" % bank)
            w_codes, w_scales = weight_mx[a, q, g]
            m_codes, m_scales = moving_mx[q, g, h]
            cols = slice(i * P, (i + 1) * P)
            nc.tensor.matmul_mx(
                out=banks[a, bank][:],
                lhsT=w_codes[:, cols].bitcast(weights[q][1]),
                lhsT_scale=w_scales[:, cols],
                rhs=m_codes[:].bitcast(movings[q][1]),
                rhs_scale=m_scales[:],
                start=first,
                stop=last,
            )

        def add_residual(a, some_banks):
            for bank in some_banks:
                i, h = bank_tiles[bank]
                part = result[a][:, i, column_half(h)]
                nc.vector.tensor_tensor(out=part, in0=banks[a, bank][:], in1=part, op=mybir.AluOpType.add)

        out_codes = keep.tile([P, ROW_GROUPS, T], U32, align_bytes=DMA_ALIGN)
        out_scales = keep.tile([P, ROW_GROUPS, T], U8, align_bytes=DMA_ALIGN)

        def round_result(engine, a, h):
            rounded[a, h] = staging_tile()
            interleave(engine, rounded[a, h], result[a][:, :, column_half(h)])

        def round_result_pair(engine, a, h, pair):
            if (a, h) not in rounded:
                rounded[a, h] = staging_tile()
            dst = rounded[a, h][:].rearrange("p (c j) -> p c j", j=PACK)
            src = result[a][:, pair, column_half(h)].rearrange("p j c -> p c j")
            copy_on[engine](out=dst[:, :, pair], in_=src)

        def quantise_result(a, h):
            nc.vector.quantize_mx(
                out=out_codes[:, a, column_half(h)].bitcast(E4M3),
                scales=out_scales[:, a, column_half(h)],
                in_=rounded[a, h][:],
            )

        for side, q, g in arrival[:-1]:
            if side == "moving":
                quantise_moving(q, g)
            else:
                for a in range(ROW_GROUPS):
                    quantise_weight(a, q, g)
        last_pass = passes[-1]
        quantise_weight(0, *last_pass)
        for pair in PAIRS:
            deal_weight("scalar", 1, *last_pass, pair)

        for q, g in passes[:-1]:
            for bank in range(BANKS):
                multiply(0, q, g, bank)
        for bank in range(BANKS):
            multiply(0, *last_pass, bank)

        add_residual(0, range(0, 3))
        round_result_pair("scalar", 0, 0, PAIRS[0])
        add_residual(0, range(3, 7))
        round_result_pair("scalar", 0, 0, PAIRS[1])
        quantise_weight_pair(1, *last_pass, slice(0, PACK))
        add_residual(0, range(7, 8))
        round_result("gpsimd", 0, 1)
        first_banks = range(0, BANKS // 2)
        for left in first_banks[::COL_HALVES]:
            for q, g in passes[:-1]:
                multiply(1, q, g, left)
                multiply(1, q, g, left + 1)
        for bank in first_banks:
            multiply(1, *last_pass, bank)
        for left in range(BANKS // 2, BANKS, COL_HALVES):
            for q, g in passes[:2]:
                multiply(1, q, g, left)
                multiply(1, q, g, left + 1)
            multiply(1, *passes[2], left)
            multiply(1, *passes[3], left)
            multiply(1, *passes[3], left + 1, closing=passes[2])
            multiply(1, *passes[2], left + 1, closing=passes[2])

        add_residual(1, range(0, 3))
        round_result_pair("scalar", 1, 0, PAIRS[0])
        add_residual(1, range(3, 4))
        round_result_pair("scalar", 1, 1, PAIRS[0])
        add_residual(1, range(4, 5))
        quantise_result(0, 0)
        quantise_result(0, 1)
        add_residual(1, range(5, 7))
        round_result_pair("scalar", 1, 0, PAIRS[1])
        add_residual(1, range(7, 8))
        round_result_pair("vector", 1, 1, PAIRS[1])
        quantise_result(1, 0)
        quantise_result(1, 1)

        def store_result(a, pair):
            nc.sync.dma_start(out=rows_on_partitions(out_0, a * SPAN)[:, pair, :], in_=result[a][:, pair, :])

        def store_codes(a, cols):
            dram = out_1[a].rearrange("p t i -> p (t i)").bitcast(I32)
            nc.sync.dma_start(out=dram[:, cols], in_=out_codes[:, a, cols].bitcast(I32))

        def store_scales():
            for row in range(4):
                dram = out_2[:, row::4, :].rearrange("a q t -> q a t").bitcast(I32)
                nc.sync.dma_start(out=dram, in_=out_scales[row:P:32].bitcast(I32))

        store_result(0, PAIRS[0])
        store_result(0, PAIRS[1])
        store_result(1, PAIRS[0])
        store_codes(0, slice(0, T))
        store_result(1, PAIRS[1])
        store_codes(1, slice(0, T))
        store_scales()
